import numpy as np
import ml_dtypes


def mxq(x, axis, fmt="e4m3"):
    dtype, down = {"e4m3": (ml_dtypes.float8_e4m3fn, 7), "e5m2": (ml_dtypes.float8_e5m2, 14)}[fmt]
    v = np.moveaxis(np.asarray(x, np.float32).astype(ml_dtypes.bfloat16).astype(np.float64), axis, -1)
    blocks = v.reshape(v.shape[:-1] + (-1, 32))
    amax = np.abs(blocks).max(-1, keepdims=True)
    byte = np.maximum(np.where(amax > 0, np.frexp(amax)[1] - 1 + 127, 0) - down, 1)
    scale = np.exp2(byte - 127.0)
    codes = (blocks / scale).astype(np.float32).astype(dtype).astype(np.float64)
    return np.moveaxis((codes * scale).reshape(v.shape), -1, axis)


WIDE = False


def mx_kscale(k):
    if not WIDE:
        return np.ones(k)
    levels = np.array([10, -10, 5, -5, 0])
    if k % 512:
        return np.exp2(np.random.permutation(np.resize(levels, k // 32))).repeat(32)
    a = np.empty((k // 512, 16))
    for p in range(k // 512):
        a[p, :8] = np.random.permutation(np.resize(levels, 8))
        for g in range(8):
            far = levels[np.abs(levels - a[p, g]) >= 10]
            a[p, g + 8] = far[np.random.randint(len(far))]
    return np.exp2(a.ravel()).repeat(32)


def f64(x):
    return np.asarray(x).astype(np.float64)


def striped(idx):
    return np.tile(idx.reshape(-1, 16).T, (8, 1)).astype(np.uint16)


def unstriped(offs):
    return offs[:16].T.reshape(-1).astype(np.int64)


E2M1 = np.array([0.0, 0.5, 1.0, 1.5, 2.0, 3.0, 4.0, 6.0, -0.0, -0.5, -1.0, -1.5, -2.0, -3.0, -4.0, -6.0])


def pack_weight(w, fmt):
    k, n = w.shape
    w = f64(np.asarray(w, np.float32).astype(ml_dtypes.bfloat16)).reshape(k // 32, 32, n)
    amax = np.abs(w).max(1)
    if fmt == "e4m3":
        byte = np.frexp(amax)[1] - 1 + 127 - 7
    else:
        mant, ex = np.frexp(amax / 6.0)
        byte = np.where(mant > 0.5, ex, ex - 1) + 127
    byte = np.clip(np.where(amax > 0, byte, 1), 1, 254)
    scaled = (w * np.exp2(127.0 - byte)[:, None, :]).reshape(k, n).astype(np.float32)
    by_word = np.ascontiguousarray(scaled.reshape(k // 512, 128, 4, n).transpose(0, 1, 3, 2))
    if fmt == "e4m3":
        words = by_word.astype(ml_dtypes.float8_e4m3fn).view(np.uint8)
    else:
        c = by_word.astype(ml_dtypes.float4_e2m1fn).view(np.uint8) & 0xF
        words = (c[..., 0::2] | (c[..., 1::2] << 4)).reshape(k // 512, 128, 2 * n)
    return np.ascontiguousarray(words), np.ascontiguousarray(byte.astype(np.uint8).reshape(k // 512, 16, n))


def unpack_weight(words, scales, fmt):
    g, _, n = scales.shape
    words = np.ascontiguousarray(words).reshape(g, 128, n, -1)
    if fmt == "e4m3":
        vals = words.view(ml_dtypes.float8_e4m3fn).astype(np.float64)
    else:
        nib = np.empty((g, 128, n, 4), np.uint8)
        nib[..., 0::2] = words & 0xF
        nib[..., 1::2] = words >> 4
        vals = E2M1[nib]
    vals = vals * np.repeat(np.exp2(scales.astype(np.float64) - 127.0), 8, axis=1)[..., None]
    return vals.transpose(0, 1, 3, 2).reshape(g * 512, n)


def gelu(v):
    return 0.5 * v * (1.0 + np.tanh(np.sqrt(2.0 / np.pi) * (v + 0.044715 * v**3)))


def twice(P):
    return np.random.permutation(np.repeat(np.arange(P), 2))


K, H, T, S, P = 1024, 512, 4096, 1024, 512


def setup_inputs():
    n = np.random.standard_normal
    s = mx_kscale(K)[:, None]
    u = mx_kscale(H)[:, None]
    d = {}
    d["tab_words"], d["tab_scales"] = pack_weight(n((K, T)) * s, "e4m3")
    d["offs"] = striped(np.random.permutation(T)[:S])
    d["pos1"] = striped(np.random.permutation(S)[:P])
    d["pos2"] = striped(np.random.permutation(S)[:P])
    d["pos3"] = striped(twice(P))
    d["w1"] = (n((K, H)) / s * u.T / K ** 0.5).astype(np.float32)
    d["w2_words"], d["w2_scales"] = pack_weight(1.4 * n((K, H)) / s / K ** 0.5, "e2m1")
    d["w3"] = (0.7 * n((K, H)) / s * u.T / K ** 0.5).astype(np.float32)
    d["w4_words"], d["w4_scales"] = pack_weight(0.7 * n((H, H)) / u / H ** 0.5, "e2m1")
    d["w5"] = (n((H, H)) / u / H ** 0.5).astype(np.float32)
    d["gh"] = (1.2 * np.exp(0.3 * n(H)) / u[:, 0]).astype(np.float32)
    return d


def reference(tab_words, tab_scales, offs, pos1, pos2, pos3, w1, w2_words, w2_scales, w3, w4_words, w4_scales, w5, gh):
    v = unpack_weight(tab_words, tab_scales, "e4m3")[:, unstriped(offs)]
    w2 = unpack_weight(w2_words, w2_scales, "e2m1")
    w4 = unpack_weight(w4_words, w4_scales, "e2m1")
    a = mxq(f64(w1), 0, "e4m3").T @ v
    b = w2.T @ v
    c = mxq(f64(w3), 0, "e4m3").T @ v
    h = a * np.tanh(b) + c
    h1 = h[:, unstriped(pos1)]
    h2 = h[:, unstriped(pos2)]
    both = mxq(h1 + h2, 0, "e4m3")
    low = mxq(np.minimum(h1, h2), 0, "e4m3")
    y = w4.T @ both - mxq(f64(w5), 0, "e4m3").T @ low
    return np.maximum(y[:, unstriped(pos3)], f64(gh)[:, None] * h)

@@ -1,0 +1,316 @@
+from contextlib import ExitStack
+
+import concourse.mybir as mybir
+
+K, H, T, S, C = 1024, 512, 4096, 1024, 512
+FLOPS = 2 * (3 * K * H * S + 2 * H * H * C)
+
+F32 = mybir.dt.float32
+BF16 = mybir.dt.bfloat16
+I32 = mybir.dt.int32
+U32 = mybir.dt.uint32
+U16 = mybir.dt.uint16
+U8 = mybir.dt.uint8
+E4M3 = mybir.dt.float8_e4m3fn_x4
+E2M1 = mybir.dt.float4_e2m1fn_x4
+ALU = mybir.AluOpType
+ACT = mybir.ActivationFunctionType
+
+P = 128
+PACK = 4
+PASSES = K // (P * PACK)
+BANK = 512
+HALVES = S // BANK
+CHUNK = 256
+GROUP = 128
+SPARE = 16
+
+
+def tile_list_amendment_clause_bundle_kernel(
+    tc, tab_words, tab_scales, offs, pos1, pos2, pos3, w1, w2_words, w2_scales, w3, w4_words, w4_scales, w5, gh, out
+):
+    nc = tc.nc
+    with ExitStack() as ctx:
+        keep = ctx.enter_context(tc.tile_pool(name="keep", bufs=1))
+        ring = ctx.enter_context(tc.tile_pool(name="ring", bufs=4))
+        psum = ctx.enter_context(tc.psum_pool(name="psum", bufs=8))
+
+        def held(name, shape, dtype):
+            return keep.tile(shape, dtype, name=name, align_bytes=64)
+
+        offs_sb = keep.tile([P, S // 16], U16, name="offs_sb")
+        pos1_sb = keep.tile([P, C // 16], U16, name="pos1_sb")
+        pos2_sb = keep.tile([P, C // 16], U16, name="pos2_sb")
+        pos3_sb = keep.tile([P, S // 16], U16, name="pos3_sb")
+        gh_sb = held("gh_sb", [P, PACK], F32)
+
+        tab_w = [held(f"tab_w{a}", [P, T], I32) for a in range(PASSES)]
+        tab_s = held("tab_s", [P, T], U8)
+        v_words = [held(f"v_words{a}", [P, S], U32) for a in range(PASSES)]
+        v_scales = [held(f"v_scales{a}", [P, S], U8) for a in range(PASSES)]
+
+        w2_raw = held("w2_raw", [P, PASSES * 2 * H], U8)
+        w2_raw_s = held("w2_raw_s", [P, PASSES * H], U8)
+        w4_raw = held("w4_raw", [P, 2 * H], U8)
+        w4_raw_s = held("w4_raw_s", [P, H], U8)
+        w2_codes = held("w2_codes", [P, PASSES * 2 * H], U8)
+        w2_sc = held("w2_sc", [P, PASSES * H], U8)
+        w4_codes = held("w4_codes", [P, 2 * H], U8)
+        w4_sc = held("w4_sc", [P, H], U8)
+
+        y = [held(f"y{t}", [P, C + SPARE], F32) for t in range(PACK)]
+
+        nc.vector.memset(tab_s[:].bitcast(I32), 0)
+        nc.gpsimd.memset(w2_raw_s[:].bitcast(I32), 0)
+        nc.gpsimd.memset(v_scales[1][:].bitcast(I32), 0)
+        nc.gpsimd.memset(w4_raw_s[:].bitcast(I32), 0)
+        for t in range(PACK):
+            nc.gpsimd.memset(y[t][:, C:], 0.0)
+
+        def table_words(a):
+            return tab_words[a].rearrange("p t i -> p (t i)").bitcast(I32)
+
+        def load_weight(name, w, a):
+            raw = held(f"{name}_raw{a}", [P, PACK, H], F32)
+            rows = w[a * P * PACK : (a + 1) * P * PACK, :]
+            nc.sync.dma_start(out=raw[:], in_=rows.rearrange("(p j) c -> p j c", j=PACK))
+            return raw
+
+        nc.sync.dma_start(offs_sb[:], offs)
+        nc.sync.dma_start(out=tab_w[0][:, : T // 4], in_=table_words(0)[:, : T // 4])
+        for q in range(4):
+            nc.sync.dma_start(
+                out=tab_s[32 * q : 32 * q + 8, :].bitcast(I32), in_=tab_scales[:, 4 * q : 4 * q + 4, :].bitcast(I32)
+            )
+        nc.sync.dma_start(out=tab_w[0][:, T // 4 :], in_=table_words(0)[:, T // 4 :])
+        nc.sync.dma_start(
+            out=w2_raw[:].bitcast(I32).rearrange("p (a n) -> p a n", a=PASSES),
+            in_=w2_words.bitcast(I32).rearrange("a p n -> p a n"),
+        )
+        for q in range(4):
+            nc.sync.dma_start(
+                out=w2_raw_s[32 * q : 32 * q + 4, :].bitcast(I32).rearrange("r (a n) -> r a n", a=PASSES),
+                in_=w2_scales[:, 4 * q : 4 * q + 4, :].bitcast(I32).rearrange("a r n -> r a n"),
+            )
+        nc.sync.dma_start(out=w4_raw[:].bitcast(I32), in_=w4_words[0].bitcast(I32))
+        for q in range(4):
+            nc.sync.dma_start(
+                out=w4_raw_s[32 * q : 32 * q + 4, :].bitcast(I32), in_=w4_scales[0, 4 * q : 4 * q + 4, :].bitcast(I32)
+            )
+        nc.sync.dma_start(out=tab_w[1][:], in_=table_words(1))
+        w1_raw = [load_weight("w1", w1, a) for a in range(PASSES)]
+        w3_raw = [load_weight("w3", w3, a) for a in range(PASSES)]
+        nc.sync.dma_start(pos1_sb[:], pos1)
+        nc.sync.dma_start(pos2_sb[:], pos2)
+        w5_raw = load_weight("w5", w5, 0)
+        nc.sync.dma_start(pos3_sb[:], pos3)
+        nc.sync.dma_start(out=gh_sb[:], in_=gh.rearrange("(p t) -> p t", t=PACK))
+
+        def deal_packed(codes, scales, raw, raw_s, passes):
+            for a in range(passes):
+                cols = slice(a * 2 * H, (a + 1) * 2 * H)
+                nc.vector.tensor_copy(
+                    out=codes[:, cols].rearrange("p (t m b) -> p t m b", t=PACK, b=2),
+                    in_=raw[:, cols].rearrange("p (m t b) -> p t m b", t=PACK, b=2),
+                )
+            nc.vector.tensor_copy(
+                out=scales[:].rearrange("p (a t m) -> p a t m", a=passes, t=PACK),
+                in_=raw_s[:].rearrange("p (a m t) -> p a t m", a=passes, t=PACK),
+            )
+
+        def weight_tiles(name):
+            return (
+                [held(f"{name}_bf{u}", [P, 2 * P * PACK], BF16) for u in range(2)],
+                [held(f"{name}_codes{u}", [P, 2 * P], U32) for u in range(2)],
+                [held(f"{name}_sc{u}", [P, 2 * P], U8) for u in range(2)],
+            )
+
+        def cast_views(raw, tiles, u):
+            dst = tiles[0][u][:].rearrange("p (e m j) -> p m j e", e=2, j=PACK)
+            src = raw[:].rearrange("p j (m u e) -> p u m j e", u=2, e=2)[:, u]
+            return dst, src
+
+        def quantize_weight(tiles, u):
+            nc.vector.quantize_mx(out=tiles[1][u][:].bitcast(E4M3), scales=tiles[2][u][:], in_=tiles[0][u][:])
+
+        def e4m3_weight(tiles, t):
+            cols = slice((t % 2) * P, (t % 2 + 1) * P)
+            return tiles[1][t // 2][:, cols].bitcast(E4M3), tiles[2][t // 2][:, cols]
+
+        def e2m1_weight(codes, scales, a, t):
+            c0 = a * H + t * P
+            return codes[:, 2 * c0 : 2 * (c0 + P)].bitcast(E2M1), scales[:, c0 : c0 + P]
+
+        def table_pass(acc, weight, a, half):
+            cols = slice(half * BANK, (half + 1) * BANK)
+            nc.tensor.matmul_mx(
+                out=acc[:],
+                lhsT=weight[0],
+                lhsT_scale=weight[1],
+                rhs=v_words[a][:, cols].bitcast(E4M3),
+                rhs_scale=v_scales[a][:, cols],
+                start=(a == 0),
+                stop=(a == PASSES - 1),
+            )
+
+        blocks = [(t, half) for t in range(PACK) for half in range(HALVES)]
+        by_half = [(t, half) for half in range(HALVES) for t in range(PACK)]
+
+        nc.vector.tensor_copy(v_scales[0][:], tab_s[:].indirect(offs_sb[:]))
+        for q in range(4):
+            nc.scalar.dma_start(
+                out=v_scales[1][32 * q : 32 * q + 4, :].bitcast(I32),
+                in_=v_scales[0][32 * q + 4 : 32 * q + 8, :].bitcast(I32),
+            )
+        nc.vector.tensor_copy(v_words[0][:], tab_w[0][:].bitcast(U32).indirect(offs_sb[:]))
+        deal_packed(w2_codes, w2_sc, w2_raw, w2_raw_s, PASSES)
+        deal_packed(w4_codes, w4_sc, w4_raw, w4_raw_s, 1)
+
+        acc_b = {}
+        for t, half in by_half:
+            acc_b[t, half] = psum.tile([P, BANK], F32, name="acc")
+            table_pass(acc_b[t, half], e2m1_weight(w2_codes, w2_sc, 0, t), 0, half)
+
+        gate = [held(f"gate{t}", [P, S], F32) for t in range(PACK)]
+        for half in range(HALVES):
+            cols = slice(half * BANK, (half + 1) * BANK)
+            ocols = slice(half * BANK // 16, (half + 1) * BANK // 16)
+            nc.vector.tensor_copy(v_words[1][:, cols], tab_w[1][:].bitcast(U32).indirect(offs_sb[:, ocols]))
+            for t in range(PACK):
+                table_pass(acc_b[t, half], e2m1_weight(w2_codes, w2_sc, 1, t), 1, half)
+                nc.scalar.activation(out=gate[t][:, cols], in_=acc_b[t, half][:], func=ACT.Tanh)
+
+        w1_q = [weight_tiles(f"w1_{a}") for a in range(PASSES)]
+        w3_q = [weight_tiles(f"w3_{a}") for a in range(PASSES)]
+        w5_q = weight_tiles("w5")
+        for a in range(PASSES):
+            for u in range(2):
+                dst, src = cast_views(w1_raw[a], w1_q[a], u)
+                nc.vector.tensor_copy(out=dst, in_=src)
+            for u in range(2):
+                quantize_weight(w1_q[a], u)
+        for a in range(PASSES):
+            for u in range(2):
+                dst, src = cast_views(w3_raw[a], w3_q[a], u)
+                nc.scalar.copy(out=dst, in_=src)
+
+        acc_a = {}
+        for t, half in by_half:
+            acc_a[t, half] = psum.tile([P, BANK], F32, name="acc")
+            table_pass(acc_a[t, half], e4m3_weight(w1_q[0], t), 0, half)
+        for t, half in blocks:
+            table_pass(acc_a[t, half], e4m3_weight(w1_q[1], t), 1, half)
+
+        def gate_block(t, half):
+            cols = slice(half * BANK, (half + 1) * BANK)
+            nc.vector.tensor_tensor(out=gate[t][:, cols], in0=acc_a[t, half][:], in1=gate[t][:, cols], op=ALU.mult)
+
+        for t, half in blocks[:4]:
+            gate_block(t, half)
+        for u in range(2):
+            quantize_weight(w3_q[0], u)
+        for t, half in blocks[4:6]:
+            gate_block(t, half)
+        quantize_weight(w3_q[1], 0)
+        for t, half in blocks[6:]:
+            gate_block(t, half)
+        quantize_weight(w3_q[1], 1)
+
+        for u in range(2):
+            dst, src = cast_views(w5_raw, w5_q, u)
+            nc.scalar.activation(out=dst, in_=src, func=ACT.Copy, scale=-1.0)
+
+        h = [held(f"feat{t}", [P, S], F32) for t in range(PACK)]
+        h1 = held("first", [P, PACK, C], F32)
+        h2 = held("second", [P, PACK, C], F32)
+
+        def features(t):
+            for half in range(HALVES):
+                cols = slice(half * BANK, (half + 1) * BANK)
+                acc = psum.tile([P, BANK], F32, name="acc")
+                for a in range(PASSES):
+                    table_pass(acc, e4m3_weight(w3_q[a], t), a, half)
+                nc.vector.tensor_tensor(out=h[t][:, cols], in0=acc[:], in1=gate[t][:, cols], op=ALU.add)
+
+        def pick(t):
+            nc.vector.tensor_copy(h1[:, t, :], h[t][:].indirect(pos1_sb[:]))
+            nc.vector.tensor_copy(h2[:, t, :], h[t][:].indirect(pos2_sb[:]))
+
+        features(0)
+        for t in range(1, PACK):
+            features(t)
+            pick(t - 1)
+        for u in range(2):
+            quantize_weight(w5_q, u)
+        pick(PACK - 1)
+
+        chunks = C // CHUNK
+        pair_bf = [held(f"pair_bf{n}", [P, 2, CHUNK * PACK], BF16) for n in range(chunks)]
+        pair_codes = [held(f"pair_codes{n}", [P, 2 * CHUNK], U32) for n in range(chunks)]
+        pair_sc = [held(f"pair_sc{n}", [P, 2 * CHUNK], U8) for n in range(chunks)]
+
+        def combine(n, which, op):
+            cols = slice(n * CHUNK, (n + 1) * CHUNK)
+            nc.vector.tensor_tensor(
+                out=pair_bf[n][:, which, :].rearrange("p (c i t) -> p c t i", i=2, t=PACK),
+                in0=h1[:, :, cols].rearrange("p t (c i) -> p c t i", i=2),
+                in1=h2[:, :, cols].rearrange("p t (c i) -> p c t i", i=2),
+                op=op,
+            )
+
+        def scores(n):
+            nc.vector.quantize_mx(
+                out=pair_codes[n][:].bitcast(E4M3),
+                scales=pair_sc[n][:],
+                in_=pair_bf[n][:].rearrange("p w x -> p (w x)"),
+            )
+            for t in range(PACK):
+                acc = psum.tile([P, BANK], F32, name="acc")
+                for g in range(CHUNK // GROUP):
+                    cols = slice(g * GROUP, (g + 1) * GROUP)
+                    for which, weight in enumerate((e2m1_weight(w4_codes, w4_sc, 0, t), e4m3_weight(w5_q, t))):
+                        src = slice(which * CHUNK + g * GROUP, which * CHUNK + (g + 1) * GROUP)
+                        nc.tensor.matmul_mx(
+                            out=acc[:, cols],
+                            lhsT=weight[0],
+                            lhsT_scale=weight[1],
+                            rhs=pair_codes[n][:, src].bitcast(E4M3),
+                            rhs_scale=pair_sc[n][:, src],
+                            start=(which == 0),
+                            stop=(which == 1),
+                        )
+                nc.scalar.copy(out=y[t][:, n * CHUNK : (n + 1) * CHUNK], in_=acc[:, :CHUNK])
+
+        combine(0, 0, ALU.add)
+        combine(0, 1, ALU.min)
+        combine(1, 0, ALU.add)
+        scores(0)
+        combine(1, 1, ALU.min)
+        scores(1)
+
+        out_rows = out.rearrange("(p t) j -> p t j", t=PACK)
+        picked = {}
+
+        def fetch(t, half):
+            ocols = slice(half * BANK // 16, (half + 1) * BANK // 16)
+            picked[t, half] = ring.tile([P, BANK], F32, name="picked")
+            nc.vector.tensor_copy(picked[t, half][:], y[t][:].indirect(pos3_sb[:, ocols]))
+
+        def finish(t, half):
+            cols = slice(half * BANK, (half + 1) * BANK)
+            res = ring.tile([P, BANK], F32, name="res")
+            nc.vector.scalar_tensor_tensor(
+                out=res[:],
+                in0=h[t][:, cols],
+                scalar=gh_sb[:, t : t + 1],
+                in1=picked[t, half][:],
+                op0=ALU.mult,
+                op1=ALU.max,
+            )
+            nc.sync.dma_start(out=out_rows[:, t, cols], in_=res[:])
+
+        fetch(*blocks[0])
+        for n in range(1, len(blocks)):
+            fetch(*blocks[n])
+            finish(*blocks[n - 1])
+        finish(*blocks[-1])

@@ -33,7 +33,7 @@ def tile_list_amendment_clause_bundle_kernel(
     with ExitStack() as ctx:
         keep = ctx.enter_context(tc.tile_pool(name="keep", bufs=1))
         ring = ctx.enter_context(tc.tile_pool(name="ring", bufs=4))
-        psum = ctx.enter_context(tc.psum_pool(name="psum", bufs=8))
+        psum = ctx.enter_context(tc.psum_pool(name="psum", bufs=4))
 
         def held(name, shape, dtype):
             return keep.tile(shape, dtype, name=name, align_bytes=64)
@@ -77,42 +77,51 @@ def tile_list_amendment_clause_bundle_kernel(
             return raw
 
         nc.sync.dma_start(offs_sb[:], offs)
+        nc.sync.dma_start(
+            out=w2_raw[:].bitcast(I32).rearrange("p (a n) -> p a n", a=PASSES),
+            in_=w2_words.bitcast(I32).rearrange("a p n -> p a n"),
+        )
+        nc.sync.dma_start(out=w4_raw[:].bitcast(I32), in_=w4_words[0].bitcast(I32))
         nc.sync.dma_start(out=tab_w[0][:, : T // 4], in_=table_words(0)[:, : T // 4])
         for q in range(4):
             nc.sync.dma_start(
                 out=tab_s[32 * q : 32 * q + 8, :].bitcast(I32), in_=tab_scales[:, 4 * q : 4 * q + 4, :].bitcast(I32)
             )
-        nc.sync.dma_start(out=tab_w[0][:, T // 4 :], in_=table_words(0)[:, T // 4 :])
-        nc.sync.dma_start(
-            out=w2_raw[:].bitcast(I32).rearrange("p (a n) -> p a n", a=PASSES),
-            in_=w2_words.bitcast(I32).rearrange("a p n -> p a n"),
-        )
+        nc.sync.dma_start(out=tab_w[0][:, T // 4 : 3 * T // 4], in_=table_words(0)[:, T // 4 : 3 * T // 4])
         for q in range(4):
             nc.sync.dma_start(
                 out=w2_raw_s[32 * q : 32 * q + 4, :].bitcast(I32).rearrange("r (a n) -> r a n", a=PASSES),
                 in_=w2_scales[:, 4 * q : 4 * q + 4, :].bitcast(I32).rearrange("a r n -> r a n"),
             )
-        nc.sync.dma_start(out=w4_raw[:].bitcast(I32), in_=w4_words[0].bitcast(I32))
+        nc.sync.dma_start(out=tab_w[0][:, 3 * T // 4 :], in_=table_words(0)[:, 3 * T // 4 :])
+        nc.sync.dma_start(out=tab_w[1][:], in_=table_words(1))
+        nc.vector.tensor_copy(v_scales[0][:], tab_s[:].indirect(offs_sb[:]))
         for q in range(4):
             nc.sync.dma_start(
-                out=w4_raw_s[32 * q : 32 * q + 4, :].bitcast(I32), in_=w4_scales[0, 4 * q : 4 * q + 4, :].bitcast(I32)
+                out=v_scales[1][32 * q : 32 * q + 4, :].bitcast(I32),
+                in_=v_scales[0][32 * q + 4 : 32 * q + 8, :].bitcast(I32),
             )
-        nc.sync.dma_start(out=tab_w[1][:], in_=table_words(1))
         w1_raw = [load_weight("w1", w1, a) for a in range(PASSES)]
         w3_raw = [load_weight("w3", w3, a) for a in range(PASSES)]
         nc.sync.dma_start(pos1_sb[:], pos1)
         nc.sync.dma_start(pos2_sb[:], pos2)
         w5_raw = load_weight("w5", w5, 0)
+        for q in range(4):
+            nc.sync.dma_start(
+                out=w4_raw_s[32 * q : 32 * q + 4, :].bitcast(I32), in_=w4_scales[0, 4 * q : 4 * q + 4, :].bitcast(I32)
+            )
         nc.sync.dma_start(pos3_sb[:], pos3)
         nc.sync.dma_start(out=gh_sb[:], in_=gh.rearrange("(p t) -> p t", t=PACK))
 
-        def deal_packed(codes, scales, raw, raw_s, passes):
+        def deal_words(codes, raw, passes):
             for a in range(passes):
                 cols = slice(a * 2 * H, (a + 1) * 2 * H)
                 nc.vector.tensor_copy(
                     out=codes[:, cols].rearrange("p (t m b) -> p t m b", t=PACK, b=2),
                     in_=raw[:, cols].rearrange("p (m t b) -> p t m b", t=PACK, b=2),
                 )
+
+        def deal_scales(scales, raw_s, passes):
             nc.vector.tensor_copy(
                 out=scales[:].rearrange("p (a t m) -> p a t m", a=passes, t=PACK),
                 in_=raw_s[:].rearrange("p (a m t) -> p a t m", a=passes, t=PACK),
@@ -154,65 +163,79 @@ def tile_list_amendment_clause_bundle_kernel(
             )
 
         blocks = [(t, half) for t in range(PACK) for half in range(HALVES)]
-        by_half = [(t, half) for half in range(HALVES) for t in range(PACK)]
+        by_pair = [(2 * u + e, half) for u in range(2) for half in range(HALVES) for e in range(2)]
 
-        nc.vector.tensor_copy(v_scales[0][:], tab_s[:].indirect(offs_sb[:]))
-        for q in range(4):
-            nc.scalar.dma_start(
-                out=v_scales[1][32 * q : 32 * q + 4, :].bitcast(I32),
-                in_=v_scales[0][32 * q + 4 : 32 * q + 8, :].bitcast(I32),
-            )
-        nc.vector.tensor_copy(v_words[0][:], tab_w[0][:].bitcast(U32).indirect(offs_sb[:]))
-        deal_packed(w2_codes, w2_sc, w2_raw, w2_raw_s, PASSES)
-        deal_packed(w4_codes, w4_sc, w4_raw, w4_raw_s, 1)
+        deal_words(w2_codes, w2_raw, PASSES)
+        deal_words(w4_codes, w4_raw, 1)
+
+        def fetch_words(a, half):
+            cols = slice(half * BANK, (half + 1) * BANK)
+            ocols = slice(half * BANK // 16, (half + 1) * BANK // 16)
+            nc.vector.tensor_copy(v_words[a][:, cols], tab_w[a][:].bitcast(U32).indirect(offs_sb[:, ocols]))
+
+        deal_scales(w2_sc, w2_raw_s, PASSES)
+        fetch_words(0, 0)
+        fetch_words(0, 1)
 
         acc_b = {}
-        for t, half in by_half:
-            acc_b[t, half] = psum.tile([P, BANK], F32, name="acc")
+        for t, half in by_pair:
+            acc_b[t, half] = psum.tile([P, BANK], F32, name=("low_banks", "high_banks")[t // 2])
             table_pass(acc_b[t, half], e2m1_weight(w2_codes, w2_sc, 0, t), 0, half)
 
         gate = [held(f"gate{t}", [P, S], F32) for t in range(PACK)]
         for half in range(HALVES):
+            fetch_words(1, half)
+        for t, half in by_pair:
             cols = slice(half * BANK, (half + 1) * BANK)
-            ocols = slice(half * BANK // 16, (half + 1) * BANK // 16)
-            nc.vector.tensor_copy(v_words[1][:, cols], tab_w[1][:].bitcast(U32).indirect(offs_sb[:, ocols]))
-            for t in range(PACK):
-                table_pass(acc_b[t, half], e2m1_weight(w2_codes, w2_sc, 1, t), 1, half)
-                nc.scalar.activation(out=gate[t][:, cols], in_=acc_b[t, half][:], func=ACT.Tanh)
+            table_pass(acc_b[t, half], e2m1_weight(w2_codes, w2_sc, 1, t), 1, half)
+            nc.scalar.activation(out=gate[t][:, cols], in_=acc_b[t, half][:], func=ACT.Tanh)
 
         w1_q = [weight_tiles(f"w1_{a}") for a in range(PASSES)]
         w3_q = [weight_tiles(f"w3_{a}") for a in range(PASSES)]
         w5_q = weight_tiles("w5")
-        for a in range(PASSES):
-            for u in range(2):
-                dst, src = cast_views(w1_raw[a], w1_q[a], u)
-                nc.vector.tensor_copy(out=dst, in_=src)
-            for u in range(2):
-                quantize_weight(w1_q[a], u)
+        for u in range(2):
+            dst, src = cast_views(w1_raw[0], w1_q[0], u)
+            nc.vector.tensor_copy(out=dst, in_=src)
+        for u in range(2):
+            quantize_weight(w1_q[0], u)
+        dst, src = cast_views(w1_raw[1], w1_q[1], 0)
+        nc.vector.tensor_copy(out=dst, in_=src)
+        quantize_weight(w1_q[1], 0)
+        dst, src = cast_views(w1_raw[1], w1_q[1], 1)
+        nc.scalar.copy(out=dst, in_=src)
         for a in range(PASSES):
             for u in range(2):
                 dst, src = cast_views(w3_raw[a], w3_q[a], u)
                 nc.scalar.copy(out=dst, in_=src)
 
         acc_a = {}
-        for t, half in by_half:
-            acc_a[t, half] = psum.tile([P, BANK], F32, name="acc")
+
+        def open_a(t, half):
+            acc_a[t, half] = psum.tile([P, BANK], F32, name="low_banks")
             table_pass(acc_a[t, half], e4m3_weight(w1_q[0], t), 0, half)
-        for t, half in blocks:
+
+        def close_a(t, half):
             table_pass(acc_a[t, half], e4m3_weight(w1_q[1], t), 1, half)
 
         def gate_block(t, half):
             cols = slice(half * BANK, (half + 1) * BANK)
             nc.vector.tensor_tensor(out=gate[t][:, cols], in0=acc_a[t, half][:], in1=gate[t][:, cols], op=ALU.mult)
 
-        for t, half in blocks[:4]:
+        for t, half in by_pair[:4]:
+            open_a(t, half)
+        for t, half in by_pair[:4]:
+            close_a(t, half)
+        quantize_weight(w1_q[1], 1)
+        for t, half in by_pair[:4]:
             gate_block(t, half)
+            open_a(t + 2, half)
+            close_a(t + 2, half)
         for u in range(2):
             quantize_weight(w3_q[0], u)
-        for t, half in blocks[4:6]:
+        for t, half in by_pair[4:6]:
             gate_block(t, half)
         quantize_weight(w3_q[1], 0)
-        for t, half in blocks[6:]:
+        for t, half in by_pair[6:]:
             gate_block(t, half)
         quantize_weight(w3_q[1], 1)
 
@@ -227,7 +250,7 @@ def tile_list_amendment_clause_bundle_kernel(
         def features(t):
             for half in range(HALVES):
                 cols = slice(half * BANK, (half + 1) * BANK)
-                acc = psum.tile([P, BANK], F32, name="acc")
+                acc = psum.tile([P, BANK], F32, name=("high_banks", "low_banks")[t // 2])
                 for a in range(PASSES):
                     table_pass(acc, e4m3_weight(w3_q[a], t), a, half)
                 nc.vector.tensor_tensor(out=h[t][:, cols], in0=acc[:], in1=gate[t][:, cols], op=ALU.add)
@@ -240,6 +263,7 @@ def tile_list_amendment_clause_bundle_kernel(
         for t in range(1, PACK):
             features(t)
             pick(t - 1)
+        deal_scales(w4_sc, w4_raw_s, 1)
         for u in range(2):
             quantize_weight(w5_q, u)
         pick(PACK - 1)
@@ -265,7 +289,7 @@ def tile_list_amendment_clause_bundle_kernel(
                 in_=pair_bf[n][:].rearrange("p w x -> p (w x)"),
             )
             for t in range(PACK):
-                acc = psum.tile([P, BANK], F32, name="acc")
+                acc = psum.tile([P, BANK], F32, name=("high_banks", "low_banks")[n])
                 for g in range(CHUNK // GROUP):
                     cols = slice(g * GROUP, (g + 1) * GROUP)
                     for which, weight in enumerate((e2m1_weight(w4_codes, w4_sc, 0, t), e4m3_weight(w5_q, t))):

@@ -21,7 +21,7 @@ PACK = 4
 PASSES = K // (P * PACK)
 BANK = 512
 HALVES = S // BANK
-CHUNK = 256
+CHUNKS = (256, 128, 128)
 GROUP = 128
 SPARE = 16
 
@@ -46,6 +46,7 @@ def tile_list_amendment_clause_bundle_kernel(
 
         tab_w = [held(f"tab_w{a}", [P, T], I32) for a in range(PASSES)]
         tab_s = held("tab_s", [P, T], U8)
+        picked_s = held("picked_s", [P, S], U8)
         v_words = [held(f"v_words{a}", [P, S], U32) for a in range(PASSES)]
         v_scales = [held(f"v_scales{a}", [P, S], U8) for a in range(PASSES)]
 
@@ -62,7 +63,8 @@ def tile_list_amendment_clause_bundle_kernel(
 
         nc.vector.memset(tab_s[:].bitcast(I32), 0)
         nc.gpsimd.memset(w2_raw_s[:].bitcast(I32), 0)
-        nc.gpsimd.memset(v_scales[1][:].bitcast(I32), 0)
+        for a in range(PASSES):
+            nc.gpsimd.memset(v_scales[a][:].bitcast(I32), 0)
         nc.gpsimd.memset(w4_raw_s[:].bitcast(I32), 0)
         for t in range(PACK):
             nc.gpsimd.memset(y[t][:, C:], 0.0)
@@ -77,30 +79,35 @@ def tile_list_amendment_clause_bundle_kernel(
             return raw
 
         nc.sync.dma_start(offs_sb[:], offs)
-        nc.sync.dma_start(
-            out=w2_raw[:].bitcast(I32).rearrange("p (a n) -> p a n", a=PASSES),
-            in_=w2_words.bitcast(I32).rearrange("a p n -> p a n"),
-        )
-        nc.sync.dma_start(out=w4_raw[:].bitcast(I32), in_=w4_words[0].bitcast(I32))
         nc.sync.dma_start(out=tab_w[0][:, : T // 4], in_=table_words(0)[:, : T // 4])
-        for q in range(4):
-            nc.sync.dma_start(
-                out=tab_s[32 * q : 32 * q + 8, :].bitcast(I32), in_=tab_scales[:, 4 * q : 4 * q + 4, :].bitcast(I32)
-            )
-        nc.sync.dma_start(out=tab_w[0][:, T // 4 : 3 * T // 4], in_=table_words(0)[:, T // 4 : 3 * T // 4])
+        nc.sync.dma_start(
+            out=tab_s[0:P:4, :].bitcast(I32), in_=tab_scales.rearrange("a q t -> (a q) t").bitcast(I32)
+        )
         for q in range(4):
             nc.sync.dma_start(
                 out=w2_raw_s[32 * q : 32 * q + 4, :].bitcast(I32).rearrange("r (a n) -> r a n", a=PASSES),
                 in_=w2_scales[:, 4 * q : 4 * q + 4, :].bitcast(I32).rearrange("a r n -> r a n"),
             )
-        nc.sync.dma_start(out=tab_w[0][:, 3 * T // 4 :], in_=table_words(0)[:, 3 * T // 4 :])
-        nc.sync.dma_start(out=tab_w[1][:], in_=table_words(1))
-        nc.vector.tensor_copy(v_scales[0][:], tab_s[:].indirect(offs_sb[:]))
-        for q in range(4):
-            nc.sync.dma_start(
-                out=v_scales[1][32 * q : 32 * q + 4, :].bitcast(I32),
-                in_=v_scales[0][32 * q + 4 : 32 * q + 8, :].bitcast(I32),
-            )
+        nc.sync.dma_start(
+            out=w2_raw[:].bitcast(I32).rearrange("p (a n) -> p a n", a=PASSES),
+            in_=w2_words.bitcast(I32).rearrange("a p n -> p a n"),
+        )
+        nc.sync.dma_start(out=tab_w[0][:, T // 4 :], in_=table_words(0)[:, T // 4 :])
+        nc.sync.dma_start(out=w4_raw[:].bitcast(I32), in_=w4_words[0].bitcast(I32))
+        nc.vector.tensor_copy(picked_s[:], tab_s[:].indirect(offs_sb[:]))
+
+        def place_scale_rows(a):
+            for q in range(4):
+                first = 64 * a + 16 * q
+                nc.sync.dma_start(
+                    out=v_scales[a][32 * q : 32 * q + 4, :].bitcast(I32),
+                    in_=picked_s[first : first + 16 : 4, :].bitcast(I32),
+                )
+
+        nc.sync.dma_start(out=tab_w[1][:, : T // 4], in_=table_words(1)[:, : T // 4])
+        place_scale_rows(0)
+        nc.sync.dma_start(out=tab_w[1][:, T // 4 :], in_=table_words(1)[:, T // 4 :])
+        place_scale_rows(1)
         w1_raw = [load_weight("w1", w1, a) for a in range(PASSES)]
         w3_raw = [load_weight("w3", w3, a) for a in range(PASSES)]
         nc.sync.dma_start(pos1_sb[:], pos1)
@@ -127,9 +134,9 @@ def tile_list_amendment_clause_bundle_kernel(
                 in_=raw_s[:].rearrange("p (a m t) -> p a t m", a=passes, t=PACK),
             )
 
-        def weight_tiles(name):
+        def weight_tiles(name, rounded):
             return (
-                [held(f"{name}_bf{u}", [P, 2 * P * PACK], BF16) for u in range(2)],
+                rounded,
                 [held(f"{name}_codes{u}", [P, 2 * P], U32) for u in range(2)],
                 [held(f"{name}_sc{u}", [P, 2 * P], U8) for u in range(2)],
             )
@@ -166,7 +173,6 @@ def tile_list_amendment_clause_bundle_kernel(
         by_pair = [(2 * u + e, half) for u in range(2) for half in range(HALVES) for e in range(2)]
 
         deal_words(w2_codes, w2_raw, PASSES)
-        deal_words(w4_codes, w4_raw, 1)
 
         def fetch_words(a, half):
             cols = slice(half * BANK, (half + 1) * BANK)
@@ -176,6 +182,7 @@ def tile_list_amendment_clause_bundle_kernel(
         deal_scales(w2_sc, w2_raw_s, PASSES)
         fetch_words(0, 0)
         fetch_words(0, 1)
+        deal_words(w4_codes, w4_raw, 1)
 
         acc_b = {}
         for t, half in by_pair:
@@ -190,9 +197,8 @@ def tile_list_amendment_clause_bundle_kernel(
             table_pass(acc_b[t, half], e2m1_weight(w2_codes, w2_sc, 1, t), 1, half)
             nc.scalar.activation(out=gate[t][:, cols], in_=acc_b[t, half][:], func=ACT.Tanh)
 
-        w1_q = [weight_tiles(f"w1_{a}") for a in range(PASSES)]
-        w3_q = [weight_tiles(f"w3_{a}") for a in range(PASSES)]
-        w5_q = weight_tiles("w5")
+        w1_q = [weight_tiles(f"w1_{a}", [held(f"w1_{a}_bf{u}", [P, 2 * P * PACK], BF16) for u in range(2)]) for a in range(PASSES)]
+        w3_q = [weight_tiles(f"w3_{a}", [held(f"w3_{a}_bf{u}", [P, 2 * P * PACK], BF16) for u in range(2)]) for a in range(PASSES)]
         for u in range(2):
             dst, src = cast_views(w1_raw[0], w1_q[0], u)
             nc.vector.tensor_copy(out=dst, in_=src)
@@ -202,7 +208,7 @@ def tile_list_amendment_clause_bundle_kernel(
         nc.vector.tensor_copy(out=dst, in_=src)
         quantize_weight(w1_q[1], 0)
         dst, src = cast_views(w1_raw[1], w1_q[1], 1)
-        nc.scalar.copy(out=dst, in_=src)
+        nc.vector.tensor_copy(out=dst, in_=src)
         for a in range(PASSES):
             for u in range(2):
                 dst, src = cast_views(w3_raw[a], w3_q[a], u)
@@ -239,10 +245,6 @@ def tile_list_amendment_clause_bundle_kernel(
             gate_block(t, half)
         quantize_weight(w3_q[1], 1)
 
-        for u in range(2):
-            dst, src = cast_views(w5_raw, w5_q, u)
-            nc.scalar.activation(out=dst, in_=src, func=ACT.Copy, scale=-1.0)
-
         h = [held(f"feat{t}", [P, S], F32) for t in range(PACK)]
         h1 = held("first", [P, PACK, C], F32)
         h2 = held("second", [P, PACK, C], F32)
@@ -253,7 +255,12 @@ def tile_list_amendment_clause_bundle_kernel(
                 acc = psum.tile([P, BANK], F32, name=("high_banks", "low_banks")[t // 2])
                 for a in range(PASSES):
                     table_pass(acc, e4m3_weight(w3_q[a], t), a, half)
-                nc.vector.tensor_tensor(out=h[t][:, cols], in0=acc[:], in1=gate[t][:, cols], op=ALU.add)
+                if t == 0:
+                    nc.vector.tensor_tensor(out=h[t][:, cols], in0=acc[:], in1=gate[t][:, cols], op=ALU.add)
+                else:
+                    c_sb = ring.tile([P, BANK], F32, name="staged", align_bytes=64)
+                    nc.scalar.copy(out=c_sb[:], in_=acc[:])
+                    nc.gpsimd.tensor_tensor(out=h[t][:, cols], in0=c_sb[:], in1=gate[t][:, cols], op=ALU.add)
 
         def pick(t):
             nc.vector.tensor_copy(h1[:, t, :], h[t][:].indirect(pos1_sb[:]))
@@ -263,18 +270,25 @@ def tile_list_amendment_clause_bundle_kernel(
         for t in range(1, PACK):
             features(t)
             pick(t - 1)
+        w5_q = weight_tiles(
+            "w5", [ring.tile([P, 2 * P * PACK], BF16, name="staged", align_bytes=64) for u in range(2)]
+        )
+        for u in range(2):
+            dst, src = cast_views(w5_raw, w5_q, u)
+            nc.scalar.activation(out=dst, in_=src, func=ACT.Copy, scale=-1.0)
+
         deal_scales(w4_sc, w4_raw_s, 1)
         for u in range(2):
             quantize_weight(w5_q, u)
         pick(PACK - 1)
 
-        chunks = C // CHUNK
-        pair_bf = [held(f"pair_bf{n}", [P, 2, CHUNK * PACK], BF16) for n in range(chunks)]
-        pair_codes = [held(f"pair_codes{n}", [P, 2 * CHUNK], U32) for n in range(chunks)]
-        pair_sc = [held(f"pair_sc{n}", [P, 2 * CHUNK], U8) for n in range(chunks)]
+        starts = [sum(CHUNKS[:n]) for n in range(len(CHUNKS))]
+        pair_bf = [held(f"pair_bf{n}", [P, 2, width * PACK], BF16) for n, width in enumerate(CHUNKS)]
+        pair_codes = [held(f"pair_codes{n}", [P, 2 * width], U32) for n, width in enumerate(CHUNKS)]
+        pair_sc = [held(f"pair_sc{n}", [P, 2 * width], U8) for n, width in enumerate(CHUNKS)]
 
         def combine(n, which, op):
-            cols = slice(n * CHUNK, (n + 1) * CHUNK)
+            cols = slice(starts[n], starts[n] + CHUNKS[n])
             nc.vector.tensor_tensor(
                 out=pair_bf[n][:, which, :].rearrange("p (c i t) -> p c t i", i=2, t=PACK),
                 in0=h1[:, :, cols].rearrange("p t (c i) -> p c t i", i=2),
@@ -283,17 +297,18 @@ def tile_list_amendment_clause_bundle_kernel(
             )
 
         def scores(n):
+            width = CHUNKS[n]
             nc.vector.quantize_mx(
                 out=pair_codes[n][:].bitcast(E4M3),
                 scales=pair_sc[n][:],
                 in_=pair_bf[n][:].rearrange("p w x -> p (w x)"),
             )
             for t in range(PACK):
-                acc = psum.tile([P, BANK], F32, name=("high_banks", "low_banks")[n])
-                for g in range(CHUNK // GROUP):
+                acc = psum.tile([P, BANK], F32, name=("high_banks", "low_banks")[n % 2])
+                for g in range(width // GROUP):
                     cols = slice(g * GROUP, (g + 1) * GROUP)
                     for which, weight in enumerate((e2m1_weight(w4_codes, w4_sc, 0, t), e4m3_weight(w5_q, t))):
-                        src = slice(which * CHUNK + g * GROUP, which * CHUNK + (g + 1) * GROUP)
+                        src = slice(which * width + g * GROUP, which * width + (g + 1) * GROUP)
                         nc.tensor.matmul_mx(
                             out=acc[:, cols],
                             lhsT=weight[0],
@@ -303,14 +318,15 @@ def tile_list_amendment_clause_bundle_kernel(
                             start=(which == 0),
                             stop=(which == 1),
                         )
-                nc.scalar.copy(out=y[t][:, n * CHUNK : (n + 1) * CHUNK], in_=acc[:, :CHUNK])
+                nc.scalar.copy(out=y[t][:, starts[n] : starts[n] + width], in_=acc[:, :width])
 
         combine(0, 0, ALU.add)
         combine(0, 1, ALU.min)
-        combine(1, 0, ALU.add)
-        scores(0)
-        combine(1, 1, ALU.min)
-        scores(1)
+        for n in range(1, len(CHUNKS)):
+            combine(n, 0, ALU.add)
+            scores(n - 1)
+            combine(n, 1, ALU.min)
+        scores(len(CHUNKS) - 1)
 
         out_rows = out.rearrange("(p t) j -> p t j", t=PACK)
         picked = {}
@@ -320,21 +336,23 @@ def tile_list_amendment_clause_bundle_kernel(
             picked[t, half] = ring.tile([P, BANK], F32, name="picked")
             nc.vector.tensor_copy(picked[t, half][:], y[t][:].indirect(pos3_sb[:, ocols]))
 
-        def finish(t, half):
-            cols = slice(half * BANK, (half + 1) * BANK)
+        def finish(t, half, pieces):
             res = ring.tile([P, BANK], F32, name="res")
-            nc.vector.scalar_tensor_tensor(
-                out=res[:],
-                in0=h[t][:, cols],
-                scalar=gh_sb[:, t : t + 1],
-                in1=picked[t, half][:],
-                op0=ALU.mult,
-                op1=ALU.max,
-            )
-            nc.sync.dma_start(out=out_rows[:, t, cols], in_=res[:])
+            width = BANK // pieces
+            for c0 in range(0, BANK, width):
+                cols = slice(half * BANK + c0, half * BANK + c0 + width)
+                nc.vector.scalar_tensor_tensor(
+                    out=res[:, c0 : c0 + width],
+                    in0=h[t][:, cols],
+                    scalar=gh_sb[:, t : t + 1],
+                    in1=picked[t, half][:, c0 : c0 + width],
+                    op0=ALU.mult,
+                    op1=ALU.max,
+                )
+                nc.sync.dma_start(out=out_rows[:, t, cols], in_=res[:, c0 : c0 + width])
 
         fetch(*blocks[0])
         for n in range(1, len(blocks)):
             fetch(*blocks[n])
-            finish(*blocks[n - 1])
-        finish(*blocks[-1])
+            finish(*blocks[n - 1], 1)
+        finish(*blocks[-1], 2)

@@ -18,12 +18,18 @@ ACT = mybir.ActivationFunctionType
 
 P = 128
 PACK = 4
+PAIRS = PACK // 2
 PASSES = K // (P * PACK)
+QUADS = 4
+LIST_ROWS = 16
 BANK = 512
 HALVES = S // BANK
+RING = 4
+TABLE_HEAD = T // 4
 CHUNKS = (256, 128, 128)
 GROUP = 128
 SPARE = 16
+LAST_PIECES = 2
 
 
 def tile_list_amendment_clause_bundle_kernel(
@@ -32,16 +38,16 @@ def tile_list_amendment_clause_bundle_kernel(
     nc = tc.nc
     with ExitStack() as ctx:
         keep = ctx.enter_context(tc.tile_pool(name="keep", bufs=1))
-        ring = ctx.enter_context(tc.tile_pool(name="ring", bufs=4))
-        psum = ctx.enter_context(tc.psum_pool(name="psum", bufs=4))
+        ring = ctx.enter_context(tc.tile_pool(name="ring", bufs=RING))
+        psum = ctx.enter_context(tc.psum_pool(name="psum", bufs=RING))
 
         def held(name, shape, dtype):
             return keep.tile(shape, dtype, name=name, align_bytes=64)
 
-        offs_sb = keep.tile([P, S // 16], U16, name="offs_sb")
-        pos1_sb = keep.tile([P, C // 16], U16, name="pos1_sb")
-        pos2_sb = keep.tile([P, C // 16], U16, name="pos2_sb")
-        pos3_sb = keep.tile([P, S // 16], U16, name="pos3_sb")
+        offs_sb = keep.tile([P, S // LIST_ROWS], U16, name="offs_sb")
+        pos1_sb = keep.tile([P, C // LIST_ROWS], U16, name="pos1_sb")
+        pos2_sb = keep.tile([P, C // LIST_ROWS], U16, name="pos2_sb")
+        pos3_sb = keep.tile([P, S // LIST_ROWS], U16, name="pos3_sb")
         gh_sb = held("gh_sb", [P, PACK], F32)
 
         tab_w = [held(f"tab_w{a}", [P, T], I32) for a in range(PASSES)]
@@ -79,11 +85,11 @@ def tile_list_amendment_clause_bundle_kernel(
             return raw
 
         nc.sync.dma_start(offs_sb[:], offs)
-        nc.sync.dma_start(out=tab_w[0][:, : T // 4], in_=table_words(0)[:, : T // 4])
+        nc.sync.dma_start(out=tab_w[0][:, : TABLE_HEAD], in_=table_words(0)[:, : TABLE_HEAD])
         nc.sync.dma_start(
             out=tab_s[0:P:4, :].bitcast(I32), in_=tab_scales.rearrange("a q t -> (a q) t").bitcast(I32)
         )
-        for q in range(4):
+        for q in range(QUADS):
             nc.sync.dma_start(
                 out=w2_raw_s[32 * q : 32 * q + 4, :].bitcast(I32).rearrange("r (a n) -> r a n", a=PASSES),
                 in_=w2_scales[:, 4 * q : 4 * q + 4, :].bitcast(I32).rearrange("a r n -> r a n"),
@@ -92,28 +98,28 @@ def tile_list_amendment_clause_bundle_kernel(
             out=w2_raw[:].bitcast(I32).rearrange("p (a n) -> p a n", a=PASSES),
             in_=w2_words.bitcast(I32).rearrange("a p n -> p a n"),
         )
-        nc.sync.dma_start(out=tab_w[0][:, T // 4 :], in_=table_words(0)[:, T // 4 :])
+        nc.sync.dma_start(out=tab_w[0][:, TABLE_HEAD:], in_=table_words(0)[:, TABLE_HEAD:])
         nc.sync.dma_start(out=w4_raw[:].bitcast(I32), in_=w4_words[0].bitcast(I32))
         nc.vector.tensor_copy(picked_s[:], tab_s[:].indirect(offs_sb[:]))
 
         def place_scale_rows(a):
-            for q in range(4):
+            for q in range(QUADS):
                 first = 64 * a + 16 * q
                 nc.sync.dma_start(
                     out=v_scales[a][32 * q : 32 * q + 4, :].bitcast(I32),
                     in_=picked_s[first : first + 16 : 4, :].bitcast(I32),
                 )
 
-        nc.sync.dma_start(out=tab_w[1][:, : T // 4], in_=table_words(1)[:, : T // 4])
+        nc.sync.dma_start(out=tab_w[1][:, : TABLE_HEAD], in_=table_words(1)[:, : TABLE_HEAD])
         place_scale_rows(0)
-        nc.sync.dma_start(out=tab_w[1][:, T // 4 :], in_=table_words(1)[:, T // 4 :])
+        nc.sync.dma_start(out=tab_w[1][:, TABLE_HEAD:], in_=table_words(1)[:, TABLE_HEAD:])
         place_scale_rows(1)
         w1_raw = [load_weight("w1", w1, a) for a in range(PASSES)]
         w3_raw = [load_weight("w3", w3, a) for a in range(PASSES)]
         nc.sync.dma_start(pos1_sb[:], pos1)
         nc.sync.dma_start(pos2_sb[:], pos2)
         w5_raw = load_weight("w5", w5, 0)
-        for q in range(4):
+        for q in range(QUADS):
             nc.sync.dma_start(
                 out=w4_raw_s[32 * q : 32 * q + 4, :].bitcast(I32), in_=w4_scales[0, 4 * q : 4 * q + 4, :].bitcast(I32)
             )
@@ -137,8 +143,8 @@ def tile_list_amendment_clause_bundle_kernel(
         def weight_tiles(name, rounded):
             return (
                 rounded,
-                [held(f"{name}_codes{u}", [P, 2 * P], U32) for u in range(2)],
-                [held(f"{name}_sc{u}", [P, 2 * P], U8) for u in range(2)],
+                [held(f"{name}_codes{u}", [P, 2 * P], U32) for u in range(PAIRS)],
+                [held(f"{name}_sc{u}", [P, 2 * P], U8) for u in range(PAIRS)],
             )
 
         def cast_views(raw, tiles, u):
@@ -170,13 +176,13 @@ def tile_list_amendment_clause_bundle_kernel(
             )
 
         blocks = [(t, half) for t in range(PACK) for half in range(HALVES)]
-        by_pair = [(2 * u + e, half) for u in range(2) for half in range(HALVES) for e in range(2)]
+        by_pair = [(2 * u + e, half) for u in range(PAIRS) for half in range(HALVES) for e in range(2)]
 
         deal_words(w2_codes, w2_raw, PASSES)
 
         def fetch_words(a, half):
             cols = slice(half * BANK, (half + 1) * BANK)
-            ocols = slice(half * BANK // 16, (half + 1) * BANK // 16)
+            ocols = slice(half * BANK // LIST_ROWS, (half + 1) * BANK // LIST_ROWS)
             nc.vector.tensor_copy(v_words[a][:, cols], tab_w[a][:].bitcast(U32).indirect(offs_sb[:, ocols]))
 
         deal_scales(w2_sc, w2_raw_s, PASSES)
@@ -197,12 +203,15 @@ def tile_list_amendment_clause_bundle_kernel(
             table_pass(acc_b[t, half], e2m1_weight(w2_codes, w2_sc, 1, t), 1, half)
             nc.scalar.activation(out=gate[t][:, cols], in_=acc_b[t, half][:], func=ACT.Tanh)
 
-        w1_q = [weight_tiles(f"w1_{a}", [held(f"w1_{a}_bf{u}", [P, 2 * P * PACK], BF16) for u in range(2)]) for a in range(PASSES)]
-        w3_q = [weight_tiles(f"w3_{a}", [held(f"w3_{a}_bf{u}", [P, 2 * P * PACK], BF16) for u in range(2)]) for a in range(PASSES)]
-        for u in range(2):
+        def held_weight(name):
+            return weight_tiles(name, [held(f"{name}_bf{u}", [P, 2 * P * PACK], BF16) for u in range(PAIRS)])
+
+        w1_q = [held_weight(f"w1_{a}") for a in range(PASSES)]
+        w3_q = [held_weight(f"w3_{a}") for a in range(PASSES)]
+        for u in range(PAIRS):
             dst, src = cast_views(w1_raw[0], w1_q[0], u)
             nc.vector.tensor_copy(out=dst, in_=src)
-        for u in range(2):
+        for u in range(PAIRS):
             quantize_weight(w1_q[0], u)
         dst, src = cast_views(w1_raw[1], w1_q[1], 0)
         nc.vector.tensor_copy(out=dst, in_=src)
@@ -210,7 +219,7 @@ def tile_list_amendment_clause_bundle_kernel(
         dst, src = cast_views(w1_raw[1], w1_q[1], 1)
         nc.vector.tensor_copy(out=dst, in_=src)
         for a in range(PASSES):
-            for u in range(2):
+            for u in range(PAIRS):
                 dst, src = cast_views(w3_raw[a], w3_q[a], u)
                 nc.scalar.copy(out=dst, in_=src)
 
@@ -227,23 +236,21 @@ def tile_list_amendment_clause_bundle_kernel(
             cols = slice(half * BANK, (half + 1) * BANK)
             nc.vector.tensor_tensor(out=gate[t][:, cols], in0=acc_a[t, half][:], in1=gate[t][:, cols], op=ALU.mult)
 
-        for t, half in by_pair[:4]:
+        for t, half in by_pair[:RING]:
             open_a(t, half)
-        for t, half in by_pair[:4]:
+        for t, half in by_pair[:RING]:
             close_a(t, half)
         quantize_weight(w1_q[1], 1)
-        for t, half in by_pair[:4]:
+        for t, half in by_pair[:RING]:
             gate_block(t, half)
             open_a(t + 2, half)
             close_a(t + 2, half)
-        for u in range(2):
+        for u in range(PAIRS):
             quantize_weight(w3_q[0], u)
-        for t, half in by_pair[4:6]:
-            gate_block(t, half)
-        quantize_weight(w3_q[1], 0)
-        for t, half in by_pair[6:]:
-            gate_block(t, half)
-        quantize_weight(w3_q[1], 1)
+        for half, u in zip(range(HALVES), range(PAIRS)):
+            for t in (2, 3):
+                gate_block(t, half)
+            quantize_weight(w3_q[1], u)
 
         h = [held(f"feat{t}", [P, S], F32) for t in range(PACK)]
         h1 = held("first", [P, PACK, C], F32)
@@ -271,44 +278,69 @@ def tile_list_amendment_clause_bundle_kernel(
             features(t)
             pick(t - 1)
         w5_q = weight_tiles(
-            "w5", [ring.tile([P, 2 * P * PACK], BF16, name="staged", align_bytes=64) for u in range(2)]
+            "w5", [ring.tile([P, 2 * P * PACK], BF16, name="staged", align_bytes=64) for u in range(PAIRS)]
         )
-        for u in range(2):
+        for u in range(PAIRS):
             dst, src = cast_views(w5_raw, w5_q, u)
             nc.scalar.activation(out=dst, in_=src, func=ACT.Copy, scale=-1.0)
 
+        h1_bf = ring.tile([P, PAIRS, 2 * C], BF16, name="staged", align_bytes=64)
+        h2_bf = ring.tile([P, PAIRS, 2 * C], BF16, name="staged", align_bytes=64)
+
+        def round_pair(dst, src, u, cols):
+            nc.scalar.copy(
+                out=dst[:, u, :].rearrange("p (c e) -> p c e", e=2)[:, cols, :],
+                in_=src[:, 2 * u : 2 * u + 2, cols].rearrange("p e c -> p c e"),
+            )
+
+        round_pair(h1_bf, h1, 0, slice(0, C))
+        round_pair(h2_bf, h2, 0, slice(0, C))
         deal_scales(w4_sc, w4_raw_s, 1)
-        for u in range(2):
+        for u in range(PAIRS):
             quantize_weight(w5_q, u)
         pick(PACK - 1)
+        round_pair(h1_bf, h1, 1, slice(0, C))
 
         starts = [sum(CHUNKS[:n]) for n in range(len(CHUNKS))]
         pair_bf = [held(f"pair_bf{n}", [P, 2, width * PACK], BF16) for n, width in enumerate(CHUNKS)]
         pair_codes = [held(f"pair_codes{n}", [P, 2 * width], U32) for n, width in enumerate(CHUNKS)]
         pair_sc = [held(f"pair_sc{n}", [P, 2 * width], U8) for n, width in enumerate(CHUNKS)]
 
-        def combine(n, which, op):
-            cols = slice(starts[n], starts[n] + CHUNKS[n])
+        chunk_cols = [slice(start, start + width) for start, width in zip(starts, CHUNKS)]
+        for cols in chunk_cols:
+            round_pair(h2_bf, h2, 1, cols)
+
+        def add_chunk(n):
             nc.vector.tensor_tensor(
-                out=pair_bf[n][:, which, :].rearrange("p (c i t) -> p c t i", i=2, t=PACK),
-                in0=h1[:, :, cols].rearrange("p t (c i) -> p c t i", i=2),
-                in1=h2[:, :, cols].rearrange("p t (c i) -> p c t i", i=2),
-                op=op,
+                out=pair_bf[n][:, 0, :].rearrange("p (c i t) -> p c t i", i=2, t=PACK),
+                in0=h1[:, :, chunk_cols[n]].rearrange("p t (c i) -> p c t i", i=2),
+                in1=h2[:, :, chunk_cols[n]].rearrange("p t (c i) -> p c t i", i=2),
+                op=ALU.add,
             )
 
-        def scores(n):
-            width = CHUNKS[n]
+        def min_chunk(n):
+            nc.vector.tensor_tensor(
+                out=pair_bf[n][:, 1, :].rearrange("p (c u e) -> p c u e", u=PAIRS, e=2),
+                in0=h1_bf[:].rearrange("p u (c e) -> p c u e", e=2)[:, chunk_cols[n]],
+                in1=h2_bf[:].rearrange("p u (c e) -> p c u e", e=2)[:, chunk_cols[n]],
+                op=ALU.min,
+            )
+
+        def quantize_chunk(n):
             nc.vector.quantize_mx(
                 out=pair_codes[n][:].bitcast(E4M3),
                 scales=pair_sc[n][:],
                 in_=pair_bf[n][:].rearrange("p w x -> p (w x)"),
             )
-            for t in range(PACK):
-                acc = psum.tile([P, BANK], F32, name=("high_banks", "low_banks")[n % 2])
-                for g in range(width // GROUP):
-                    cols = slice(g * GROUP, (g + 1) * GROUP)
+
+        def scores(t, chunks, banks):
+            acc = psum.tile([P, BANK], F32, name=banks)
+            first = min(starts[n] for n in chunks)
+            for n in chunks:
+                for g in range(0, CHUNKS[n], GROUP):
+                    cols = slice(starts[n] - first + g, starts[n] - first + g + GROUP)
                     for which, weight in enumerate((e2m1_weight(w4_codes, w4_sc, 0, t), e4m3_weight(w5_q, t))):
-                        src = slice(which * width + g * GROUP, which * width + (g + 1) * GROUP)
+                        src = slice(which * CHUNKS[n] + g, which * CHUNKS[n] + g + GROUP)
                         nc.tensor.matmul_mx(
                             out=acc[:, cols],
                             lhsT=weight[0],
@@ -318,21 +350,26 @@ def tile_list_amendment_clause_bundle_kernel(
                             start=(which == 0),
                             stop=(which == 1),
                         )
-                nc.scalar.copy(out=y[t][:, starts[n] : starts[n] + width], in_=acc[:, :width])
+            width = sum(CHUNKS[n] for n in chunks)
+            nc.scalar.copy(out=y[t][:, first : first + width], in_=acc[:, :width])
 
-        combine(0, 0, ALU.add)
-        combine(0, 1, ALU.min)
+        add_chunk(0)
+        min_chunk(0)
         for n in range(1, len(CHUNKS)):
-            combine(n, 0, ALU.add)
-            scores(n - 1)
-            combine(n, 1, ALU.min)
-        scores(len(CHUNKS) - 1)
+            add_chunk(n)
+            quantize_chunk(n - 1)
+            min_chunk(n)
+        quantize_chunk(len(CHUNKS) - 1)
+        for n in range(len(CHUNKS)):
+            scores(0, [n], "high_banks")
+        for t in range(1, PACK):
+            scores(t, range(len(CHUNKS) - 1, -1, -1), "low_banks")
 
         out_rows = out.rearrange("(p t) j -> p t j", t=PACK)
         picked = {}
 
         def fetch(t, half):
-            ocols = slice(half * BANK // 16, (half + 1) * BANK // 16)
+            ocols = slice(half * BANK // LIST_ROWS, (half + 1) * BANK // LIST_ROWS)
             picked[t, half] = ring.tile([P, BANK], F32, name="picked")
             nc.vector.tensor_copy(picked[t, half][:], y[t][:].indirect(pos3_sb[:, ocols]))
 
@@ -355,4 +392,4 @@ def tile_list_amendment_clause_bundle_kernel(
         for n in range(1, len(blocks)):
             fetch(*blocks[n])
             finish(*blocks[n - 1], 1)
-        finish(*blocks[-1], 2)
+        finish(*blocks[-1], LAST_PIECES)

from contextlib import ExitStack

import concourse.mybir as mybir

K, H, T, S, C = 1024, 512, 4096, 1024, 512
FLOPS = 2 * (3 * K * H * S + 2 * H * H * C)

F32 = mybir.dt.float32
BF16 = mybir.dt.bfloat16
I32 = mybir.dt.int32
U32 = mybir.dt.uint32
U16 = mybir.dt.uint16
U8 = mybir.dt.uint8
E4M3 = mybir.dt.float8_e4m3fn_x4
E2M1 = mybir.dt.float4_e2m1fn_x4
ALU = mybir.AluOpType
ACT = mybir.ActivationFunctionType

P = 128
PACK = 4
PAIRS = PACK // 2
PASSES = K // (P * PACK)
QUADS = 4
LIST_ROWS = 16
BANK = 512
HALVES = S // BANK
RING = 4
TABLE_HEAD = T // 4
CHUNKS = (256, 128, 128)
GROUP = 128
SPARE = 16
LAST_PIECES = 2


def tile_list_amendment_clause_bundle_kernel(
    tc, tab_words, tab_scales, offs, pos1, pos2, pos3, w1, w2_words, w2_scales, w3, w4_words, w4_scales, w5, gh, out
):
    nc = tc.nc
    with ExitStack() as ctx:
        keep = ctx.enter_context(tc.tile_pool(name="keep", bufs=1))
        ring = ctx.enter_context(tc.tile_pool(name="ring", bufs=RING))
        psum = ctx.enter_context(tc.psum_pool(name="psum", bufs=RING))

        def held(name, shape, dtype):
            return keep.tile(shape, dtype, name=name, align_bytes=64)

        offs_sb = keep.tile([P, S // LIST_ROWS], U16, name="offs_sb")
        pos1_sb = keep.tile([P, C // LIST_ROWS], U16, name="pos1_sb")
        pos2_sb = keep.tile([P, C // LIST_ROWS], U16, name="pos2_sb")
        pos3_sb = keep.tile([P, S // LIST_ROWS], U16, name="pos3_sb")
        gh_sb = held("gh_sb", [P, PACK], F32)

        tab_w = [held(f"tab_w{a}", [P, T], I32) for a in range(PASSES)]
        tab_s = held("tab_s", [P, T], U8)
        picked_s = held("picked_s", [P, S], U8)
        v_words = [held(f"v_words{a}", [P, S], U32) for a in range(PASSES)]
        v_scales = [held(f"v_scales{a}", [P, S], U8) for a in range(PASSES)]

        w2_raw = held("w2_raw", [P, PASSES * 2 * H], U8)
        w2_raw_s = held("w2_raw_s", [P, PASSES * H], U8)
        w4_raw = held("w4_raw", [P, 2 * H], U8)
        w4_raw_s = held("w4_raw_s", [P, H], U8)
        w2_codes = held("w2_codes", [P, PASSES * 2 * H], U8)
        w2_sc = held("w2_sc", [P, PASSES * H], U8)
        w4_codes = held("w4_codes", [P, 2 * H], U8)
        w4_sc = held("w4_sc", [P, H], U8)

        y = [held(f"y{t}", [P, C + SPARE], F32) for t in range(PACK)]

        nc.vector.memset(tab_s[:].bitcast(I32), 0)
        nc.gpsimd.memset(w2_raw_s[:].bitcast(I32), 0)
        for a in range(PASSES):
            nc.gpsimd.memset(v_scales[a][:].bitcast(I32), 0)
        nc.gpsimd.memset(w4_raw_s[:].bitcast(I32), 0)
        for t in range(PACK):
            nc.gpsimd.memset(y[t][:, C:], 0.0)

        def table_words(a):
            return tab_words[a].rearrange("p t i -> p (t i)").bitcast(I32)

        def load_weight(name, w, a):
            raw = held(f"{name}_raw{a}", [P, PACK, H], F32)
            rows = w[a * P * PACK : (a + 1) * P * PACK, :]
            nc.sync.dma_start(out=raw[:], in_=rows.rearrange("(p j) c -> p j c", j=PACK))
            return raw

        nc.sync.dma_start(offs_sb[:], offs)
        nc.sync.dma_start(out=tab_w[0][:, : TABLE_HEAD], in_=table_words(0)[:, : TABLE_HEAD])
        nc.sync.dma_start(
            out=tab_s[0:P:4, :].bitcast(I32), in_=tab_scales.rearrange("a q t -> (a q) t").bitcast(I32)
        )
        for q in range(QUADS):
            nc.sync.dma_start(
                out=w2_raw_s[32 * q : 32 * q + 4, :].bitcast(I32).rearrange("r (a n) -> r a n", a=PASSES),
                in_=w2_scales[:, 4 * q : 4 * q + 4, :].bitcast(I32).rearrange("a r n -> r a n"),
            )
        nc.sync.dma_start(
            out=w2_raw[:].bitcast(I32).rearrange("p (a n) -> p a n", a=PASSES),
            in_=w2_words.bitcast(I32).rearrange("a p n -> p a n"),
        )
        nc.sync.dma_start(out=tab_w[0][:, TABLE_HEAD:], in_=table_words(0)[:, TABLE_HEAD:])
        nc.sync.dma_start(out=w4_raw[:].bitcast(I32), in_=w4_words[0].bitcast(I32))
        nc.vector.tensor_copy(picked_s[:], tab_s[:].indirect(offs_sb[:]))

        def place_scale_rows(a):
            for q in range(QUADS):
                first = 64 * a + 16 * q
                nc.sync.dma_start(
                    out=v_scales[a][32 * q : 32 * q + 4, :].bitcast(I32),
                    in_=picked_s[first : first + 16 : 4, :].bitcast(I32),
                )

        nc.sync.dma_start(out=tab_w[1][:, : TABLE_HEAD], in_=table_words(1)[:, : TABLE_HEAD])
        place_scale_rows(0)
        nc.sync.dma_start(out=tab_w[1][:, TABLE_HEAD:], in_=table_words(1)[:, TABLE_HEAD:])
        place_scale_rows(1)
        w1_raw = [load_weight("w1", w1, a) for a in range(PASSES)]
        w3_raw = [load_weight("w3", w3, a) for a in range(PASSES)]
        nc.sync.dma_start(pos1_sb[:], pos1)
        nc.sync.dma_start(pos2_sb[:], pos2)
        w5_raw = load_weight("w5", w5, 0)
        for q in range(QUADS):
            nc.sync.dma_start(
                out=w4_raw_s[32 * q : 32 * q + 4, :].bitcast(I32), in_=w4_scales[0, 4 * q : 4 * q + 4, :].bitcast(I32)
            )
        nc.sync.dma_start(pos3_sb[:], pos3)
        nc.sync.dma_start(out=gh_sb[:], in_=gh.rearrange("(p t) -> p t", t=PACK))

        def deal_words(codes, raw, passes):
            for a in range(passes):
                cols = slice(a * 2 * H, (a + 1) * 2 * H)
                nc.vector.tensor_copy(
                    out=codes[:, cols].rearrange("p (t m b) -> p t m b", t=PACK, b=2),
                    in_=raw[:, cols].rearrange("p (m t b) -> p t m b", t=PACK, b=2),
                )

        def deal_scales(scales, raw_s, passes):
            nc.vector.tensor_copy(
                out=scales[:].rearrange("p (a t m) -> p a t m", a=passes, t=PACK),
                in_=raw_s[:].rearrange("p (a m t) -> p a t m", a=passes, t=PACK),
            )

        def weight_tiles(name, rounded):
            return (
                rounded,
                [held(f"{name}_codes{u}", [P, 2 * P], U32) for u in range(PAIRS)],
                [held(f"{name}_sc{u}", [P, 2 * P], U8) for u in range(PAIRS)],
            )

        def cast_views(raw, tiles, u):
            dst = tiles[0][u][:].rearrange("p (e m j) -> p m j e", e=2, j=PACK)
            src = raw[:].rearrange("p j (m u e) -> p u m j e", u=2, e=2)[:, u]
            return dst, src

        def quantize_weight(tiles, u):
            nc.vector.quantize_mx(out=tiles[1][u][:].bitcast(E4M3), scales=tiles[2][u][:], in_=tiles[0][u][:])

        def e4m3_weight(tiles, t):
            cols = slice((t % 2) * P, (t % 2 + 1) * P)
            return tiles[1][t // 2][:, cols].bitcast(E4M3), tiles[2][t // 2][:, cols]

        def e2m1_weight(codes, scales, a, t):
            c0 = a * H + t * P
            return codes[:, 2 * c0 : 2 * (c0 + P)].bitcast(E2M1), scales[:, c0 : c0 + P]

        def table_pass(acc, weight, a, half):
            cols = slice(half * BANK, (half + 1) * BANK)
            nc.tensor.matmul_mx(
                out=acc[:],
                lhsT=weight[0],
                lhsT_scale=weight[1],
                rhs=v_words[a][:, cols].bitcast(E4M3),
                rhs_scale=v_scales[a][:, cols],
                start=(a == 0),
                stop=(a == PASSES - 1),
            )

        blocks = [(t, half) for t in range(PACK) for half in range(HALVES)]
        by_pair = [(2 * u + e, half) for u in range(PAIRS) for half in range(HALVES) for e in range(2)]

        deal_words(w2_codes, w2_raw, PASSES)

        def fetch_words(a, half):
            cols = slice(half * BANK, (half + 1) * BANK)
            ocols = slice(half * BANK // LIST_ROWS, (half + 1) * BANK // LIST_ROWS)
            nc.vector.tensor_copy(v_words[a][:, cols], tab_w[a][:].bitcast(U32).indirect(offs_sb[:, ocols]))

        deal_scales(w2_sc, w2_raw_s, PASSES)
        fetch_words(0, 0)
        fetch_words(0, 1)
        deal_words(w4_codes, w4_raw, 1)

        acc_b = {}
        for t, half in by_pair:
            acc_b[t, half] = psum.tile([P, BANK], F32, name=("low_banks", "high_banks")[t // 2])
            table_pass(acc_b[t, half], e2m1_weight(w2_codes, w2_sc, 0, t), 0, half)

        gate = [held(f"gate{t}", [P, S], F32) for t in range(PACK)]
        for half in range(HALVES):
            fetch_words(1, half)
        for t, half in by_pair:
            cols = slice(half * BANK, (half + 1) * BANK)
            table_pass(acc_b[t, half], e2m1_weight(w2_codes, w2_sc, 1, t), 1, half)
            nc.scalar.activation(out=gate[t][:, cols], in_=acc_b[t, half][:], func=ACT.Tanh)

        def held_weight(name):
            return weight_tiles(name, [held(f"{name}_bf{u}", [P, 2 * P * PACK], BF16) for u in range(PAIRS)])

        w1_q = [held_weight(f"w1_{a}") for a in range(PASSES)]
        w3_q = [held_weight(f"w3_{a}") for a in range(PASSES)]
        for u in range(PAIRS):
            dst, src = cast_views(w1_raw[0], w1_q[0], u)
            nc.vector.tensor_copy(out=dst, in_=src)
        for u in range(PAIRS):
            quantize_weight(w1_q[0], u)
        dst, src = cast_views(w1_raw[1], w1_q[1], 0)
        nc.vector.tensor_copy(out=dst, in_=src)
        quantize_weight(w1_q[1], 0)
        dst, src = cast_views(w1_raw[1], w1_q[1], 1)
        nc.vector.tensor_copy(out=dst, in_=src)
        for a in range(PASSES):
            for u in range(PAIRS):
                dst, src = cast_views(w3_raw[a], w3_q[a], u)
                nc.scalar.copy(out=dst, in_=src)

        acc_a = {}

        def open_a(t, half):
            acc_a[t, half] = psum.tile([P, BANK], F32, name="low_banks")
            table_pass(acc_a[t, half], e4m3_weight(w1_q[0], t), 0, half)

        def close_a(t, half):
            table_pass(acc_a[t, half], e4m3_weight(w1_q[1], t), 1, half)

        def gate_block(t, half):
            cols = slice(half * BANK, (half + 1) * BANK)
            nc.vector.tensor_tensor(out=gate[t][:, cols], in0=acc_a[t, half][:], in1=gate[t][:, cols], op=ALU.mult)

        for t, half in by_pair[:RING]:
            open_a(t, half)
        for t, half in by_pair[:RING]:
            close_a(t, half)
        quantize_weight(w1_q[1], 1)
        for t, half in by_pair[:RING]:
            gate_block(t, half)
            open_a(t + 2, half)
            close_a(t + 2, half)
        for u in range(PAIRS):
            quantize_weight(w3_q[0], u)
        for half, u in zip(range(HALVES), range(PAIRS)):
            for t in (2, 3):
                gate_block(t, half)
            quantize_weight(w3_q[1], u)

        h = [held(f"feat{t}", [P, S], F32) for t in range(PACK)]
        h1 = held("first", [P, PACK, C], F32)
        h2 = held("second", [P, PACK, C], F32)

        def features(t):
            for half in range(HALVES):
                cols = slice(half * BANK, (half + 1) * BANK)
                acc = psum.tile([P, BANK], F32, name=("high_banks", "low_banks")[t // 2])
                for a in range(PASSES):
                    table_pass(acc, e4m3_weight(w3_q[a], t), a, half)
                if t == 0:
                    nc.vector.tensor_tensor(out=h[t][:, cols], in0=acc[:], in1=gate[t][:, cols], op=ALU.add)
                else:
                    c_sb = ring.tile([P, BANK], F32, name="staged", align_bytes=64)
                    nc.scalar.copy(out=c_sb[:], in_=acc[:])
                    nc.gpsimd.tensor_tensor(out=h[t][:, cols], in0=c_sb[:], in1=gate[t][:, cols], op=ALU.add)

        def pick(t):
            nc.vector.tensor_copy(h1[:, t, :], h[t][:].indirect(pos1_sb[:]))
            nc.vector.tensor_copy(h2[:, t, :], h[t][:].indirect(pos2_sb[:]))

        features(0)
        for t in range(1, PACK):
            features(t)
            pick(t - 1)
        w5_q = weight_tiles(
            "w5", [ring.tile([P, 2 * P * PACK], BF16, name="staged", align_bytes=64) for u in range(PAIRS)]
        )
        for u in range(PAIRS):
            dst, src = cast_views(w5_raw, w5_q, u)
            nc.scalar.activation(out=dst, in_=src, func=ACT.Copy, scale=-1.0)

        h1_bf = ring.tile([P, PAIRS, 2 * C], BF16, name="staged", align_bytes=64)
        h2_bf = ring.tile([P, PAIRS, 2 * C], BF16, name="staged", align_bytes=64)

        def round_pair(dst, src, u, cols):
            nc.scalar.copy(
                out=dst[:, u, :].rearrange("p (c e) -> p c e", e=2)[:, cols, :],
                in_=src[:, 2 * u : 2 * u + 2, cols].rearrange("p e c -> p c e"),
            )

        round_pair(h1_bf, h1, 0, slice(0, C))
        round_pair(h2_bf, h2, 0, slice(0, C))
        deal_scales(w4_sc, w4_raw_s, 1)
        for u in range(PAIRS):
            quantize_weight(w5_q, u)
        pick(PACK - 1)
        round_pair(h1_bf, h1, 1, slice(0, C))

        starts = [sum(CHUNKS[:n]) for n in range(len(CHUNKS))]
        pair_bf = [held(f"pair_bf{n}", [P, 2, width * PACK], BF16) for n, width in enumerate(CHUNKS)]
        pair_codes = [held(f"pair_codes{n}", [P, 2 * width], U32) for n, width in enumerate(CHUNKS)]
        pair_sc = [held(f"pair_sc{n}", [P, 2 * width], U8) for n, width in enumerate(CHUNKS)]

        chunk_cols = [slice(start, start + width) for start, width in zip(starts, CHUNKS)]
        for cols in chunk_cols:
            round_pair(h2_bf, h2, 1, cols)

        def add_chunk(n):
            nc.vector.tensor_tensor(
                out=pair_bf[n][:, 0, :].rearrange("p (c i t) -> p c t i", i=2, t=PACK),
                in0=h1[:, :, chunk_cols[n]].rearrange("p t (c i) -> p c t i", i=2),
                in1=h2[:, :, chunk_cols[n]].rearrange("p t (c i) -> p c t i", i=2),
                op=ALU.add,
            )

        def min_chunk(n):
            nc.vector.tensor_tensor(
                out=pair_bf[n][:, 1, :].rearrange("p (c u e) -> p c u e", u=PAIRS, e=2),
                in0=h1_bf[:].rearrange("p u (c e) -> p c u e", e=2)[:, chunk_cols[n]],
                in1=h2_bf[:].rearrange("p u (c e) -> p c u e", e=2)[:, chunk_cols[n]],
                op=ALU.min,
            )

        def quantize_chunk(n):
            nc.vector.quantize_mx(
                out=pair_codes[n][:].bitcast(E4M3),
                scales=pair_sc[n][:],
                in_=pair_bf[n][:].rearrange("p w x -> p (w x)"),
            )

        def scores(t, chunks, banks):
            acc = psum.tile([P, BANK], F32, name=banks)
            first = min(starts[n] for n in chunks)
            for n in chunks:
                for g in range(0, CHUNKS[n], GROUP):
                    cols = slice(starts[n] - first + g, starts[n] - first + g + GROUP)
                    for which, weight in enumerate((e2m1_weight(w4_codes, w4_sc, 0, t), e4m3_weight(w5_q, t))):
                        src = slice(which * CHUNKS[n] + g, which * CHUNKS[n] + g + GROUP)
                        nc.tensor.matmul_mx(
                            out=acc[:, cols],
                            lhsT=weight[0],
                            lhsT_scale=weight[1],
                            rhs=pair_codes[n][:, src].bitcast(E4M3),
                            rhs_scale=pair_sc[n][:, src],
                            start=(which == 0),
                            stop=(which == 1),
                        )
            width = sum(CHUNKS[n] for n in chunks)
            nc.scalar.copy(out=y[t][:, first : first + width], in_=acc[:, :width])

        add_chunk(0)
        min_chunk(0)
        for n in range(1, len(CHUNKS)):
            add_chunk(n)
            quantize_chunk(n - 1)
            min_chunk(n)
        quantize_chunk(len(CHUNKS) - 1)
        for n in range(len(CHUNKS)):
            scores(0, [n], "high_banks")
        for t in range(1, PACK):
            scores(t, range(len(CHUNKS) - 1, -1, -1), "low_banks")

        out_rows = out.rearrange("(p t) j -> p t j", t=PACK)
        picked = {}

        def fetch(t, half):
            ocols = slice(half * BANK // LIST_ROWS, (half + 1) * BANK // LIST_ROWS)
            picked[t, half] = ring.tile([P, BANK], F32, name="picked")
            nc.vector.tensor_copy(picked[t, half][:], y[t][:].indirect(pos3_sb[:, ocols]))

        def finish(t, half, pieces):
            res = ring.tile([P, BANK], F32, name="res")
            width = BANK // pieces
            for c0 in range(0, BANK, width):
                cols = slice(half * BANK + c0, half * BANK + c0 + width)
                nc.vector.scalar_tensor_tensor(
                    out=res[:, c0 : c0 + width],
                    in0=h[t][:, cols],
                    scalar=gh_sb[:, t : t + 1],
                    in1=picked[t, half][:, c0 : c0 + width],
                    op0=ALU.mult,
                    op1=ALU.max,
                )
                nc.sync.dma_start(out=out_rows[:, t, cols], in_=res[:, c0 : c0 + width])

        fetch(*blocks[0])
        for n in range(1, len(blocks)):
            fetch(*blocks[n])
            finish(*blocks[n - 1], 1)
        finish(*blocks[-1], LAST_PIECES)
